import numpy as np
import ml_dtypes


def mxq(x, axis, fmt="e4m3"):
    dtype, down = {"e4m3": (ml_dtypes.float8_e4m3fn, 7), "e5m2": (ml_dtypes.float8_e5m2, 14)}[fmt]
    v = np.moveaxis(np.asarray(x, np.float32).astype(ml_dtypes.bfloat16).astype(np.float64), axis, -1)
    blocks = v.reshape(v.shape[:-1] + (-1, 32))
    amax = np.abs(blocks).max(-1, keepdims=True)
    byte = np.maximum(np.where(amax > 0, np.frexp(amax)[1] - 1 + 127, 0) - down, 1)
    scale = np.exp2(byte - 127.0)
    codes = (blocks / scale).astype(np.float32).astype(dtype).astype(np.float64)
    return np.moveaxis((codes * scale).reshape(v.shape), -1, axis)


WIDE = False


def mx_kscale(k):
    if not WIDE:
        return np.ones(k)
    levels = np.array([10, -10, 5, -5, 0])
    if k % 512:
        return np.exp2(np.random.permutation(np.resize(levels, k // 32))).repeat(32)
    a = np.empty((k // 512, 16))
    for p in range(k // 512):
        a[p, :8] = np.random.permutation(np.resize(levels, 8))
        for g in range(8):
            far = levels[np.abs(levels - a[p, g]) >= 10]
            a[p, g + 8] = far[np.random.randint(len(far))]
    return np.exp2(a.ravel()).repeat(32)


def f64(x):
    return np.asarray(x).astype(np.float64)


def striped(idx):
    return np.tile(idx.reshape(-1, 16).T, (8, 1)).astype(np.uint16)


def unstriped(offs):
    return offs[:16].T.reshape(-1).astype(np.int64)


def pack_weight(w):
    k, n = w.shape
    w = f64(np.asarray(w, np.float32).astype(ml_dtypes.bfloat16)).reshape(k // 32, 32, n)
    amax = np.abs(w).max(1)
    byte = np.clip(np.where(amax > 0, np.frexp(amax)[1] - 1 + 127 - 7, 1), 1, 254)
    scaled = (w * np.exp2(127.0 - byte)[:, None, :]).reshape(k, n).astype(np.float32)
    words = np.ascontiguousarray(scaled.reshape(k // 512, 128, 4, n).transpose(0, 1, 3, 2)).astype(ml_dtypes.float8_e4m3fn).view(np.uint8)
    return words, np.ascontiguousarray(byte.astype(np.uint8).reshape(k // 512, 16, n))


def unpack_weight(words, scales):
    g, p, n, _ = words.shape
    vals = np.ascontiguousarray(words).view(ml_dtypes.float8_e4m3fn).astype(np.float64) * np.repeat(np.exp2(scales.astype(np.float64) - 127.0), 8, axis=1)[..., None]
    return vals.transpose(0, 1, 3, 2).reshape(g * 512, n)


E2M1 = np.array([0.0, 0.5, 1.0, 1.5, 2.0, 3.0, 4.0, 6.0, -0.0, -0.5, -1.0, -1.5, -2.0, -3.0, -4.0, -6.0])


def pack_fp4(w):
    k, n = w.shape
    w = f64(np.asarray(w, np.float32).astype(ml_dtypes.bfloat16)).reshape(k // 32, 32, n)
    amax = np.abs(w).max(1)
    mant, ex = np.frexp(amax / 6.0)
    byte = np.clip(np.where(amax > 0, np.where(mant > 0.5, ex, ex - 1) + 127, 1), 1, 254)
    scaled = (w * np.exp2(127.0 - byte)[:, None, :]).reshape(k, n).astype(np.float32)
    c = np.ascontiguousarray(scaled.reshape(k // 512, 128, 4, n).transpose(0, 1, 3, 2)).astype(ml_dtypes.float4_e2m1fn).view(np.uint8) & 0xF
    words = (c[..., 0::2] | (c[..., 1::2] << 4)).reshape(k // 512, 128, 2 * n)
    return np.ascontiguousarray(words), np.ascontiguousarray(byte.astype(np.uint8).reshape(k // 512, 16, n))


def unpack_fp4(words, scales):
    g, _, n = scales.shape
    words = np.ascontiguousarray(words).reshape(g, 128, n, 2)
    nib = np.empty((g, 128, n, 4), np.uint8)
    nib[..., 0::2] = words & 0xF
    nib[..., 1::2] = words >> 4
    vals = E2M1[nib] * np.repeat(np.exp2(scales.astype(np.float64) - 127.0), 8, axis=1)[..., None]
    return vals.transpose(0, 1, 3, 2).reshape(g * 512, n)


K, T, S, N, H = 512, 1024, 512, 128, 512


def setup_inputs():
    n = np.random.standard_normal
    s = mx_kscale(K)[:, None]
    u = mx_kscale(H)
    packed_xT = pack_weight(n((K, T)) * s)
    packed_w1 = pack_fp4(n((K, H)) / np.sqrt(K) / s)
    packed_w2 = pack_fp4(n((H, N)) / np.sqrt(H) / u[:, None])
    return {
        "x_words": packed_xT[0],
        "x_scales": packed_xT[1],
        "w1_words": packed_w1[0],
        "w1_scales": packed_w1[1],
        "unit": (np.random.uniform(0.6, 1.4, (H, 1)) * u[:, None]).astype(np.float32),
        "w2_words": packed_w2[0],
        "w2_scales": packed_w2[1],
        "offs": striped(np.random.permutation(T)[:S]),
        "d1": striped(np.random.permutation(S)),
        "d2": striped(np.random.permutation(S)),
    }


def reference(x_words, x_scales, w1_words, w1_scales, unit, w2_words, w2_scales, offs, d1, d2):
    xq = unpack_weight(x_words, x_scales)[:, unstriped(offs)]
    y = unpack_fp4(w1_words, w1_scales).T @ xq
    s1 = y[:, unstriped(d1)]
    ad = y * s1
    st = ad + ad[:, unstriped(d2)]
    ex = np.exp(1.5 * np.tanh(st))
    pr = ex / ex.mean(axis=1, keepdims=True)
    hid = f64(unit) * (pr * y - y[:, unstriped(d1)])
    return unpack_fp4(w2_words, w2_scales).T @ mxq(hid, 0, "e4m3")

@@ -1,0 +1,209 @@
+from contextlib import ExitStack
+
+import concourse.mybir as mybir
+
+K, T, S, H, N = 512, 1024, 512, 512, 128
+FLOPS = 2 * K * H * S + 2 * H * N * S
+
+F32 = mybir.dt.float32
+BF16 = mybir.dt.bfloat16
+I32 = mybir.dt.int32
+U32 = mybir.dt.uint32
+U16 = mybir.dt.uint16
+U8 = mybir.dt.uint8
+FP8X4 = mybir.dt.float8_e4m3fn_x4
+FP4X4 = mybir.dt.float4_e2m1fn_x4
+ALU = mybir.AluOpType
+ACT = mybir.ActivationFunctionType
+
+P = 128
+PACK = 4
+WINDOW = 704
+HALF = S // 2
+VECTOR_COLS = 64
+
+
+def load_scale_rows(nc, plane, rows):
+    for q in range(4):
+        nc.sync.dma_start(plane[32 * q : 32 * q + 4, :].bitcast(I32), rows[4 * q : 4 * q + 4, :].bitcast(I32))
+
+
+def tile_picked_yanti_gap_p_kernel(
+    tc, x_words, x_scales, w1_words, w1_scales, unit, w2_words, w2_scales, offs, d1, d2, out
+):
+    nc = tc.nc
+    with ExitStack() as ctx:
+        sb = ctx.enter_context(tc.tile_pool(name="sb", bufs=1))
+        ps = ctx.enter_context(tc.psum_pool(name="ps", bufs=1))
+
+        offs_t = sb.tile([P, S // 16], U16, name="offs_t")
+        d1_t = sb.tile([P, S // 16], U16, name="d1_t")
+        d2_t = sb.tile([P, S // 16], U16, name="d2_t")
+        xw = sb.tile([P, T], I32, name="xw", align_bytes=64)
+        xs = sb.tile([P, T], U8, name="xs", align_bytes=64)
+        w1w = sb.tile([P, 2 * H], U8, name="w1w", align_bytes=64)
+        w1s = sb.tile([P, H], U8, name="w1s", align_bytes=64)
+        w2w = sb.tile([P, 2 * N], U8, name="w2w", align_bytes=64)
+        w2s = sb.tile([P, N], U8, name="w2s", align_bytes=64)
+        u = sb.tile([P, PACK], F32, name="u")
+        neg_u = sb.tile([P, PACK], F32, name="neg_u")
+
+        nc.vector.memset(xs[:].bitcast(I32), 0)
+        nc.gpsimd.memset(w1s[:].bitcast(I32), 0)
+        nc.gpsimd.memset(w2s[:].bitcast(I32), 0)
+
+        nc.sync.dma_start(offs_t[:], offs)
+        nc.scalar.dma_start(xw[:], x_words[0].rearrange("p c r -> p (c r)").bitcast(I32))
+        load_scale_rows(nc, xs, x_scales[0])
+        nc.sync.dma_start(w1w[:].bitcast(I32), w1_words[0].bitcast(I32))
+        load_scale_rows(nc, w1s, w1_scales[0])
+        nc.sync.dma_start(d1_t[:], d1)
+        nc.sync.dma_start(u[:], unit.rearrange("(p t) o -> p (t o)", t=PACK))
+        nc.sync.dma_start(d2_t[:], d2)
+        nc.sync.dma_start(w2w[:].bitcast(I32), w2_words[0].bitcast(I32))
+        load_scale_rows(nc, w2s, w2_scales[0])
+
+        gw = sb.tile([P, S], U32, name="gw", align_bytes=64)
+        gs = sb.tile([P, S], U8, name="gs", align_bytes=64)
+        nc.vector.tensor_copy(gs[:], xs[:].indirect(offs_t[:]))
+
+        w1w_t = w1w[:].rearrange("p (m t b) -> p t m b", t=PACK, b=2)
+        w1s_t = w1s[:].rearrange("p (m t) -> p t m", t=PACK)
+        first_w = sb.tile([P, 1, P, 2], U8, name="first_w", align_bytes=64)
+        first_s = sb.tile([P, 1, P], U8, name="first_s", align_bytes=64)
+        rest_w = sb.tile([P, PACK - 1, P, 2], U8, name="rest_w", align_bytes=64)
+        rest_s = sb.tile([P, PACK - 1, P], U8, name="rest_s", align_bytes=64)
+        nc.vector.tensor_copy(first_w[:], w1w_t[:, 0:1])
+        nc.vector.tensor_copy(gw[:], xw[:].bitcast(U32).indirect(offs_t[:]))
+        nc.vector.tensor_copy(first_s[:], w1s_t[:, 0:1])
+        nc.vector.tensor_copy(rest_w[:], w1w_t[:, 1:PACK])
+        nc.vector.tensor_copy(rest_s[:], w1s_t[:, 1:PACK])
+
+        nc.scalar.activation(neg_u[:], u[:], ACT.Copy, scale=-1.0)
+
+        banks = [ps.tile([P, S], F32, name=f"y_bank{t}") for t in range(PACK)]
+        for t in range(PACK):
+            words = first_w[:, 0] if t == 0 else rest_w[:, t - 1]
+            scales = first_s[:, 0] if t == 0 else rest_s[:, t - 1]
+            nc.tensor.matmul_mx(
+                out=banks[t][:],
+                lhsT=words.rearrange("p m b -> p (m b)").bitcast(FP4X4),
+                lhsT_scale=scales,
+                rhs=gw[:].bitcast(FP8X4),
+                rhs_scale=gs[:],
+                start=True,
+                stop=True,
+            )
+
+        y = [sb.tile([P, WINDOW], F32, name=f"y{t}") for t in range(PACK)]
+        s1 = [sb.tile([P, S], F32, name=f"s1_{t}") for t in range(PACK)]
+        ad = [sb.tile([P, WINDOW], F32, name=f"ad{t}") for t in range(PACK)]
+        ad2 = [sb.tile([P, S], F32, name=f"ad_copy{t}") for t in range(PACK)]
+        st = [sb.tile([P, S], F32, name=f"st{t}") for t in range(PACK)]
+        th = [sb.tile([P, S], F32, name=f"th{t}") for t in range(PACK)]
+        ex = [sb.tile([P, S], F32, name=f"ex{t}") for t in range(PACK)]
+        wy = [sb.tile([P, S], F32, name=f"wy{t}") for t in range(PACK)]
+        tot = [sb.tile([P, 1], F32, name=f"tot{t}") for t in range(PACK)]
+        inv = [sb.tile([P, 1], F32, name=f"inv{t}") for t in range(PACK)]
+        fac = [sb.tile([P, 1], F32, name=f"fac{t}") for t in range(PACK)]
+        hid = sb.tile([P, PACK, S], BF16, name="hid", align_bytes=64)
+
+        def evac(t):
+            nc.scalar.activation(y[t][:, :S], banks[t][:], ACT.Copy)
+
+        def partner(t):
+            if t == 0:
+                nc.vector.tensor_copy(s1[t][:], y[t][:].indirect(d1_t[:]))
+            else:
+                nc.scalar.activation(s1[t][:], y[t][:].indirect(d1_t[:]), ACT.Copy)
+
+        def product(t):
+            nc.vector.tensor_tensor(ad[t][:, :S], banks[t][:], s1[t][:], ALU.mult)
+
+        def dup(t):
+            if t == 0:
+                nc.vector.tensor_copy(ad2[t][:], ad[t][:, :S])
+            else:
+                nc.scalar.activation(ad2[t][:], ad[t][:, :S], ACT.Copy)
+
+        def stride_sum(t):
+            nc.vector.tensor_tensor(st[t][:], ad[t][:].indirect(d2_t[:]), ad2[t][:], ALU.add)
+
+        def bounded_exp(t):
+            nc.scalar.activation(th[t][:], st[t][:], ACT.Tanh)
+            nc.scalar.activation(ex[t][:], th[t][:], ACT.Exp, scale=1.5, accum_out=tot[t][:])
+
+        def factor(t):
+            nc.vector.reciprocal(inv[t][:], tot[t][:])
+            nc.vector.tensor_scalar(fac[t][:], inv[t][:], neg_u[:, t : t + 1], -float(S), ALU.mult, ALU.mult)
+
+        def weigh(t):
+            nc.vector.scalar_tensor_tensor(wy[t][:], ex[t][:], fac[t][:], banks[t][:], ALU.mult, ALU.mult)
+
+        def hidden(t):
+            nc.vector.scalar_tensor_tensor(hid[:, t, :], s1[t][:], neg_u[:, t : t + 1], wy[t][:], ALU.mult, ALU.add)
+
+        evac(0)
+        partner(0)
+        evac(1)
+        partner(1)
+        product(0)
+        dup(0)
+        stride_sum(0)
+        evac(2)
+        partner(2)
+        product(1)
+        dup(1)
+        product(2)
+        evac(3)
+        stride_sum(1)
+        dup(2)
+        partner(3)
+        stride_sum(2)
+        bounded_exp(0)
+        product(3)
+        dup(3)
+        factor(0)
+        weigh(0)
+        stride_sum(3)
+        bounded_exp(1)
+        hidden(0)
+        for t in range(1, PACK):
+            if t + 1 < PACK:
+                bounded_exp(t + 1)
+            factor(t)
+            weigh(t)
+            hidden(t)
+
+        woven = [sb.tile([P, HALF, PACK], BF16, name=f"woven{h}", align_bytes=64) for h in range(2)]
+        hw = [sb.tile([P, HALF], U32, name=f"hw{h}", align_bytes=64) for h in range(2)]
+        hs = [sb.tile([P, HALF], U8, name=f"hs{h}", align_bytes=64) for h in range(2)]
+        res = [sb.tile([P, HALF], F32, name=f"res{h}") for h in range(2)]
+        obank = [ps.tile([P, S], F32, name=f"o_bank{h}") for h in range(2)]
+
+        def weave(copy, h, c0, c1):
+            copy(
+                woven[h][:, c0:c1, :].rearrange("p (c i) t -> p c t i", i=4),
+                hid[:, :, h * HALF + c0 : h * HALF + c1].rearrange("p t (c i) -> p c t i", i=4),
+            )
+
+        weave(nc.vector.tensor_copy, 0, 0, HALF)
+        weave(nc.scalar.copy, 1, VECTOR_COLS, HALF)
+        weave(nc.vector.tensor_copy, 1, 0, VECTOR_COLS)
+        for h in range(2):
+            nc.vector.quantize_mx(
+                out=hw[h][:].bitcast(FP8X4), scales=hs[h][:], in_=woven[h][:].rearrange("p c t -> p (c t)")
+            )
+            nc.tensor.matmul_mx(
+                out=obank[h][:, :HALF],
+                lhsT=w2w[:].bitcast(FP4X4),
+                lhsT_scale=w2s[:],
+                rhs=hw[h][:].bitcast(FP8X4),
+                rhs_scale=hs[h][:],
+                start=True,
+                stop=True,
+            )
+        nc.scalar.copy(res[0][:], obank[0][:, :HALF])
+        nc.sync.dma_start(out[:, :HALF], res[0][:])
+        nc.vector.tensor_copy(res[1][:], obank[1][:, :HALF])
+        nc.sync.dma_start(out[:, HALF:], res[1][:])

@@ -20,12 +20,19 @@ P = 128
 PACK = 4
 WINDOW = 704
 HALF = S // 2
-VECTOR_COLS = 64
+CHUNKS = [256, 128, 128]
+SCALAR_COLS = 192
+PARTNER = "VSSS"
+STRIDE = ["FV","FV","PSV","FV"]
+SKEW = 0.6
 
 
-def load_scale_rows(nc, plane, rows):
-    for q in range(4):
-        nc.sync.dma_start(plane[32 * q : 32 * q + 4, :].bitcast(I32), rows[4 * q : 4 * q + 4, :].bitcast(I32))
+def load_scale_rows(queues, plane, rows):
+    for q, queue in enumerate(queues):
+        words = rows[4 * q : 4 * q + 4, :].bitcast(I32)
+        queue.dma_start(
+            plane[32 * q : 32 * q + 32, :].bitcast(I32), words.unsqueeze(0).to_broadcast([8, 4, words.shape[1]])
+        )
 
 
 def tile_picked_yanti_gap_p_kernel(
@@ -42,26 +49,22 @@ def tile_picked_yanti_gap_p_kernel(
         xw = sb.tile([P, T], I32, name="xw", align_bytes=64)
         xs = sb.tile([P, T], U8, name="xs", align_bytes=64)
         w1w = sb.tile([P, 2 * H], U8, name="w1w", align_bytes=64)
-        w1s = sb.tile([P, H], U8, name="w1s", align_bytes=64)
+        w1s = sb.tile([P, H], U8, name="w1s", tag="w1_bytes", align_bytes=64)
         w2w = sb.tile([P, 2 * N], U8, name="w2w", align_bytes=64)
         w2s = sb.tile([P, N], U8, name="w2s", align_bytes=64)
         u = sb.tile([P, PACK], F32, name="u")
         neg_u = sb.tile([P, PACK], F32, name="neg_u")
 
-        nc.vector.memset(xs[:].bitcast(I32), 0)
-        nc.gpsimd.memset(w1s[:].bitcast(I32), 0)
-        nc.gpsimd.memset(w2s[:].bitcast(I32), 0)
-
         nc.sync.dma_start(offs_t[:], offs)
+        load_scale_rows([nc.sync, nc.scalar, nc.sync, nc.scalar], xs, x_scales[0])
         nc.scalar.dma_start(xw[:], x_words[0].rearrange("p c r -> p (c r)").bitcast(I32))
-        load_scale_rows(nc, xs, x_scales[0])
         nc.sync.dma_start(w1w[:].bitcast(I32), w1_words[0].bitcast(I32))
-        load_scale_rows(nc, w1s, w1_scales[0])
+        load_scale_rows([nc.sync] * 4, w1s, w1_scales[0])
         nc.sync.dma_start(d1_t[:], d1)
         nc.sync.dma_start(u[:], unit.rearrange("(p t) o -> p (t o)", t=PACK))
         nc.sync.dma_start(d2_t[:], d2)
         nc.sync.dma_start(w2w[:].bitcast(I32), w2_words[0].bitcast(I32))
-        load_scale_rows(nc, w2s, w2_scales[0])
+        load_scale_rows([nc.sync] * 4, w2s, w2_scales[0])
 
         gw = sb.tile([P, S], U32, name="gw", align_bytes=64)
         gs = sb.tile([P, S], U8, name="gs", align_bytes=64)
@@ -71,29 +74,36 @@ def tile_picked_yanti_gap_p_kernel(
         w1s_t = w1s[:].rearrange("p (m t) -> p t m", t=PACK)
         first_w = sb.tile([P, 1, P, 2], U8, name="first_w", align_bytes=64)
         first_s = sb.tile([P, 1, P], U8, name="first_s", align_bytes=64)
-        rest_w = sb.tile([P, PACK - 1, P, 2], U8, name="rest_w", align_bytes=64)
-        rest_s = sb.tile([P, PACK - 1, P], U8, name="rest_s", align_bytes=64)
         nc.vector.tensor_copy(first_w[:], w1w_t[:, 0:1])
         nc.vector.tensor_copy(gw[:], xw[:].bitcast(U32).indirect(offs_t[:]))
         nc.vector.tensor_copy(first_s[:], w1s_t[:, 0:1])
-        nc.vector.tensor_copy(rest_w[:], w1w_t[:, 1:PACK])
+        rest_s = sb.tile([P, PACK - 1, P], U8, name="rest_s", align_bytes=64)
         nc.vector.tensor_copy(rest_s[:], w1s_t[:, 1:PACK])
+        rest_w = sb.tile([P, PACK - 1, P, 2], U8, name="rest_w", tag="w1_bytes", align_bytes=64)
+        nc.vector.tensor_copy(rest_w[:], w1w_t[:, 1:PACK])
 
         nc.scalar.activation(neg_u[:], u[:], ACT.Copy, scale=-1.0)
 
-        banks = [ps.tile([P, S], F32, name=f"y_bank{t}") for t in range(PACK)]
-        for t in range(PACK):
+        def first_product(bank, t, cols):
             words = first_w[:, 0] if t == 0 else rest_w[:, t - 1]
             scales = first_s[:, 0] if t == 0 else rest_s[:, t - 1]
             nc.tensor.matmul_mx(
-                out=banks[t][:],
+                out=bank,
                 lhsT=words.rearrange("p m b -> p (m b)").bitcast(FP4X4),
                 lhsT_scale=scales,
-                rhs=gw[:].bitcast(FP8X4),
-                rhs_scale=gs[:],
+                rhs=gw[:, cols].bitcast(FP8X4),
+                rhs_scale=gs[:, cols],
                 start=True,
                 stop=True,
             )
+
+        halves = [slice(0, HALF), slice(HALF, S)]
+        half_banks = [ps.tile([P, HALF], F32, name=f"y0_bank{h}") for h in range(2)]
+        banks = [None] + [ps.tile([P, S], F32, name=f"y_bank{t}") for t in range(1, PACK)]
+        for h in range(2):
+            first_product(half_banks[h][:], 0, halves[h])
+        for t in range(1, PACK):
+            first_product(banks[t][:], t, slice(0, S))
 
         y = [sb.tile([P, WINDOW], F32, name=f"y{t}") for t in range(PACK)]
         s1 = [sb.tile([P, S], F32, name=f"s1_{t}") for t in range(PACK)]
@@ -109,101 +119,100 @@ def tile_picked_yanti_gap_p_kernel(
         hid = sb.tile([P, PACK, S], BF16, name="hid", align_bytes=64)
 
         def evac(t):
-            nc.scalar.activation(y[t][:, :S], banks[t][:], ACT.Copy)
+            if t == 0:
+                for h in range(2):
+                    nc.scalar.activation(y[0][:, halves[h]], half_banks[h][:], ACT.Copy)
+            else:
+                nc.scalar.activation(y[t][:, :S], banks[t][:], ACT.Copy)
+
+        def y_rows(t):
+            return y[0][:, :S] if t == 0 else banks[t][:]
 
         def partner(t):
-            if t == 0:
+            if PARTNER[t] == "V":
                 nc.vector.tensor_copy(s1[t][:], y[t][:].indirect(d1_t[:]))
             else:
                 nc.scalar.activation(s1[t][:], y[t][:].indirect(d1_t[:]), ACT.Copy)
 
         def product(t):
-            nc.vector.tensor_tensor(ad[t][:, :S], banks[t][:], s1[t][:], ALU.mult)
+            nc.vector.tensor_tensor(ad[t][:, :S], y_rows(t), s1[t][:], ALU.mult)
 
         def dup(t):
-            if t == 0:
+            if STRIDE[t] == "FV":
                 nc.vector.tensor_copy(ad2[t][:], ad[t][:, :S])
-            else:
+            elif STRIDE[t] == "FS":
                 nc.scalar.activation(ad2[t][:], ad[t][:, :S], ACT.Copy)
+            elif STRIDE[t] == "FD":
+                nc.sync.dma_start(ad2[t][:], ad[t][:, :S])
+            elif STRIDE[t][:2] == "PS":
+                nc.scalar.activation(ad2[t][:], ad[t][:].indirect(d2_t[:]), ACT.Copy)
+            else:
+                nc.vector.tensor_copy(ad2[t][:], ad[t][:].indirect(d2_t[:]))
 
         def stride_sum(t):
-            nc.vector.tensor_tensor(st[t][:], ad[t][:].indirect(d2_t[:]), ad2[t][:], ALU.add)
+            if STRIDE[t][0] == "F":
+                nc.vector.tensor_tensor(st[t][:], ad[t][:].indirect(d2_t[:]), ad2[t][:], ALU.add)
+            elif STRIDE[t][2] == "G":
+                nc.gpsimd.tensor_tensor(st[t][:], ad[t][:, :S], ad2[t][:], ALU.add)
+            else:
+                nc.vector.tensor_tensor(st[t][:], ad[t][:, :S], ad2[t][:], ALU.add)
 
-        def bounded_exp(t):
+        def bound(t):
             nc.scalar.activation(th[t][:], st[t][:], ACT.Tanh)
+
+        def exponential(t):
             nc.scalar.activation(ex[t][:], th[t][:], ACT.Exp, scale=1.5, accum_out=tot[t][:])
 
-        def factor(t):
+        def inverse(t):
             nc.vector.reciprocal(inv[t][:], tot[t][:])
+
+        def factor(t):
             nc.vector.tensor_scalar(fac[t][:], inv[t][:], neg_u[:, t : t + 1], -float(S), ALU.mult, ALU.mult)
 
         def weigh(t):
-            nc.vector.scalar_tensor_tensor(wy[t][:], ex[t][:], fac[t][:], banks[t][:], ALU.mult, ALU.mult)
+            nc.vector.scalar_tensor_tensor(wy[t][:], ex[t][:], fac[t][:], y_rows(t), ALU.mult, ALU.mult)
 
         def hidden(t):
             nc.vector.scalar_tensor_tensor(hid[:, t, :], s1[t][:], neg_u[:, t : t + 1], wy[t][:], ALU.mult, ALU.add)
 
-        evac(0)
-        partner(0)
-        evac(1)
-        partner(1)
-        product(0)
-        dup(0)
-        stride_sum(0)
-        evac(2)
-        partner(2)
-        product(1)
-        dup(1)
-        product(2)
-        evac(3)
-        stride_sum(1)
-        dup(2)
-        partner(3)
-        stride_sum(2)
-        bounded_exp(0)
-        product(3)
-        dup(3)
-        factor(0)
-        weigh(0)
-        stride_sum(3)
-        bounded_exp(1)
-        hidden(0)
-        for t in range(1, PACK):
-            if t + 1 < PACK:
-                bounded_exp(t + 1)
-            factor(t)
-            weigh(t)
-            hidden(t)
+        stages = [evac, partner, product, dup, stride_sum, bound, exponential, inverse, factor, weigh, hidden]
+        steps = [(i + SKEW * t, t, i) for t in range(PACK) for i in range(len(stages))]
+        for step in sorted(steps):
+            stages[step[2]](step[1])
 
-        woven = [sb.tile([P, HALF, PACK], BF16, name=f"woven{h}", align_bytes=64) for h in range(2)]
-        hw = [sb.tile([P, HALF], U32, name=f"hw{h}", align_bytes=64) for h in range(2)]
-        hs = [sb.tile([P, HALF], U8, name=f"hs{h}", align_bytes=64) for h in range(2)]
-        res = [sb.tile([P, HALF], F32, name=f"res{h}") for h in range(2)]
-        obank = [ps.tile([P, S], F32, name=f"o_bank{h}") for h in range(2)]
+        woven = sb.tile([P, S, PACK], BF16, name="woven", align_bytes=64)
+        hw = sb.tile([P, S], U32, name="hw", align_bytes=64)
+        hs = sb.tile([P, S], U8, name="hs", align_bytes=64)
 
-        def weave(copy, h, c0, c1):
+        def weave(copy, c0, c1):
             copy(
-                woven[h][:, c0:c1, :].rearrange("p (c i) t -> p c t i", i=4),
-                hid[:, :, h * HALF + c0 : h * HALF + c1].rearrange("p t (c i) -> p c t i", i=4),
+                woven[:, c0:c1, :].rearrange("p (c i) t -> p c t i", i=4),
+                hid[:, :, c0:c1].rearrange("p t (c i) -> p c t i", i=4),
             )
 
-        weave(nc.vector.tensor_copy, 0, 0, HALF)
-        weave(nc.scalar.copy, 1, VECTOR_COLS, HALF)
-        weave(nc.vector.tensor_copy, 1, 0, VECTOR_COLS)
-        for h in range(2):
+        weave(nc.vector.tensor_copy, 0, HALF)
+        weave(nc.scalar.copy, HALF, HALF + SCALAR_COLS)
+        weave(nc.vector.tensor_copy, HALF + SCALAR_COLS, S)
+        c0 = 0
+        for k, width in enumerate(CHUNKS):
+            cols = slice(c0, c0 + width)
             nc.vector.quantize_mx(
-                out=hw[h][:].bitcast(FP8X4), scales=hs[h][:], in_=woven[h][:].rearrange("p c t -> p (c t)")
+                out=hw[:, cols].bitcast(FP8X4), scales=hs[:, cols], in_=woven[:, cols, :].rearrange("p c t -> p (c t)")
             )
+            obank = ps.tile([P, width], F32, name=f"o_bank{k}")
             nc.tensor.matmul_mx(
-                out=obank[h][:, :HALF],
+                out=obank[:],
                 lhsT=w2w[:].bitcast(FP4X4),
                 lhsT_scale=w2s[:],
-                rhs=hw[h][:].bitcast(FP8X4),
-                rhs_scale=hs[h][:],
+                rhs=hw[:, cols].bitcast(FP8X4),
+                rhs_scale=hs[:, cols],
                 start=True,
                 stop=True,
             )
-        nc.scalar.copy(res[0][:], obank[0][:, :HALF])
-        nc.sync.dma_start(out[:, :HALF], res[0][:])
-        nc.vector.tensor_copy(res[1][:], obank[1][:, :HALF])
-        nc.sync.dma_start(out[:, HALF:], res[1][:])
+            res = sb.tile([P, width], F32, name=f"res{k}")
+            if k + 1 < len(CHUNKS):
+                nc.scalar.copy(res[:], obank[:])
+            else:
+                nc.vector.tensor_copy(res[:], obank[:])
+            nc.sync.dma_start(out[:, cols], res[:])
+            c0 = c0 + width

@@ -21,7 +21,6 @@ PACK = 4
 WINDOW = 704
 HALF = S // 2
 CHUNKS = [256, 128, 128]
-SCALAR_COLS = 192
 PARTNER = "VSSS"
 STRIDE = ["FV","FV","PSV","FV"]
 SKEW = 0.6
@@ -54,11 +53,12 @@ def tile_picked_yanti_gap_p_kernel(
         w2s = sb.tile([P, N], U8, name="w2s", align_bytes=64)
         u = sb.tile([P, PACK], F32, name="u")
         neg_u = sb.tile([P, PACK], F32, name="neg_u")
+        u_times_s = sb.tile([P, PACK], F32, name="u_times_s")
 
         nc.sync.dma_start(offs_t[:], offs)
         load_scale_rows([nc.sync, nc.scalar, nc.sync, nc.scalar], xs, x_scales[0])
-        nc.scalar.dma_start(xw[:], x_words[0].rearrange("p c r -> p (c r)").bitcast(I32))
         nc.sync.dma_start(w1w[:].bitcast(I32), w1_words[0].bitcast(I32))
+        nc.scalar.dma_start(xw[:], x_words[0].rearrange("p c r -> p (c r)").bitcast(I32))
         load_scale_rows([nc.sync] * 4, w1s, w1_scales[0])
         nc.sync.dma_start(d1_t[:], d1)
         nc.sync.dma_start(u[:], unit.rearrange("(p t) o -> p (t o)", t=PACK))
@@ -72,21 +72,22 @@ def tile_picked_yanti_gap_p_kernel(
 
         w1w_t = w1w[:].rearrange("p (m t b) -> p t m b", t=PACK, b=2)
         w1s_t = w1s[:].rearrange("p (m t) -> p t m", t=PACK)
-        first_w = sb.tile([P, 1, P, 2], U8, name="first_w", align_bytes=64)
-        first_s = sb.tile([P, 1, P], U8, name="first_s", align_bytes=64)
-        nc.vector.tensor_copy(first_w[:], w1w_t[:, 0:1])
+        first_w = sb.tile([P, 2, P, 2], U8, name="first_w", align_bytes=64)
+        first_s = sb.tile([P, 2, P], U8, name="first_s", align_bytes=64)
+        nc.vector.tensor_copy(first_w[:], w1w_t[:, 0:2])
         nc.vector.tensor_copy(gw[:], xw[:].bitcast(U32).indirect(offs_t[:]))
-        nc.vector.tensor_copy(first_s[:], w1s_t[:, 0:1])
-        rest_s = sb.tile([P, PACK - 1, P], U8, name="rest_s", align_bytes=64)
-        nc.vector.tensor_copy(rest_s[:], w1s_t[:, 1:PACK])
-        rest_w = sb.tile([P, PACK - 1, P, 2], U8, name="rest_w", tag="w1_bytes", align_bytes=64)
-        nc.vector.tensor_copy(rest_w[:], w1w_t[:, 1:PACK])
+        nc.vector.tensor_copy(first_s[:], w1s_t[:, 0:2])
+        rest_s = sb.tile([P, 2, P], U8, name="rest_s", align_bytes=64)
+        nc.vector.tensor_copy(rest_s[:], w1s_t[:, 2:PACK])
+        rest_w = sb.tile([P, 2, P, 2], U8, name="rest_w", tag="w1_bytes", align_bytes=64)
+        nc.vector.tensor_copy(rest_w[:], w1w_t[:, 2:PACK])
 
         nc.scalar.activation(neg_u[:], u[:], ACT.Copy, scale=-1.0)
+        nc.scalar.activation(u_times_s[:], u[:], ACT.Copy, scale=float(S))
 
         def first_product(bank, t, cols):
-            words = first_w[:, 0] if t == 0 else rest_w[:, t - 1]
-            scales = first_s[:, 0] if t == 0 else rest_s[:, t - 1]
+            words = first_w[:, t] if t < 2 else rest_w[:, t - 2]
+            scales = first_s[:, t] if t < 2 else rest_s[:, t - 2]
             nc.tensor.matmul_mx(
                 out=bank,
                 lhsT=words.rearrange("p m b -> p (m b)").bitcast(FP4X4),
@@ -113,10 +114,10 @@ def tile_picked_yanti_gap_p_kernel(
         th = [sb.tile([P, S], F32, name=f"th{t}") for t in range(PACK)]
         ex = [sb.tile([P, S], F32, name=f"ex{t}") for t in range(PACK)]
         wy = [sb.tile([P, S], F32, name=f"wy{t}") for t in range(PACK)]
-        tot = [sb.tile([P, 1], F32, name=f"tot{t}") for t in range(PACK)]
-        inv = [sb.tile([P, 1], F32, name=f"inv{t}") for t in range(PACK)]
-        fac = [sb.tile([P, 1], F32, name=f"fac{t}") for t in range(PACK)]
-        hid = sb.tile([P, PACK, S], BF16, name="hid", align_bytes=64)
+        tot = sb.tile([P, PACK], F32, name="tot")
+        inv = sb.tile([P, PACK], F32, name="inv")
+        fac = sb.tile([P, PACK], F32, name="fac")
+        hid = sb.tile([P, 2, PACK, HALF], BF16, name="hid", align_bytes=64)
 
         def evac(t):
             if t == 0:
@@ -161,43 +162,77 @@ def tile_picked_yanti_gap_p_kernel(
             nc.scalar.activation(th[t][:], st[t][:], ACT.Tanh)
 
         def exponential(t):
-            nc.scalar.activation(ex[t][:], th[t][:], ACT.Exp, scale=1.5, accum_out=tot[t][:])
+            nc.scalar.activation(ex[t][:], th[t][:], ACT.Exp, scale=1.5, accum_out=tot[:, t : t + 1])
+
+        def factor_cols(t):
+            return slice(0, 2) if t == 1 else slice(t, t + 1)
 
         def inverse(t):
-            nc.vector.reciprocal(inv[t][:], tot[t][:])
+            if t > 0:
+                nc.vector.reciprocal(inv[:, factor_cols(t)], tot[:, factor_cols(t)])
 
         def factor(t):
-            nc.vector.tensor_scalar(fac[t][:], inv[t][:], neg_u[:, t : t + 1], -float(S), ALU.mult, ALU.mult)
+            if t > 0:
+                nc.vector.tensor_tensor(fac[:, factor_cols(t)], inv[:, factor_cols(t)], u_times_s[:, factor_cols(t)], ALU.mult)
+
+        def weigh_cols(t, cols):
+            nc.vector.scalar_tensor_tensor(
+                wy[t][:, cols], ex[t][:, cols], fac[:, t : t + 1], y_rows(t)[:, cols], ALU.mult, ALU.mult
+            )
+
+        def hidden_half(t, h):
+            nc.vector.scalar_tensor_tensor(
+                hid[:, h, t, :], s1[t][:, halves[h]], neg_u[:, t : t + 1], wy[t][:, halves[h]], ALU.mult, ALU.add
+            )
 
         def weigh(t):
-            nc.vector.scalar_tensor_tensor(wy[t][:], ex[t][:], fac[t][:], y_rows(t), ALU.mult, ALU.mult)
+            if t == 1:
+                weigh_cols(0, slice(0, S))
+                weigh_cols(1, slice(0, S))
+            elif t > 1:
+                weigh_cols(t, halves[0])
 
         def hidden(t):
-            nc.vector.scalar_tensor_tensor(hid[:, t, :], s1[t][:], neg_u[:, t : t + 1], wy[t][:], ALU.mult, ALU.add)
+            if t == 1:
+                for k in range(2):
+                    nc.vector.scalar_tensor_tensor(
+                        hid[:, :, k, :],
+                        s1[k][:].rearrange("p (h c) -> p h c", h=2),
+                        neg_u[:, k : k + 1],
+                        wy[k][:].rearrange("p (h c) -> p h c", h=2),
+                        ALU.mult,
+                        ALU.add,
+                    )
+            elif t > 1:
+                hidden_half(t, 0)
 
         stages = [evac, partner, product, dup, stride_sum, bound, exponential, inverse, factor, weigh, hidden]
         steps = [(i + SKEW * t, t, i) for t in range(PACK) for i in range(len(stages))]
         for step in sorted(steps):
             stages[step[2]](step[1])
 
-        woven = sb.tile([P, S, PACK], BF16, name="woven", align_bytes=64)
+        woven = [sb.tile([P, width, PACK], BF16, name=f"woven{k}", align_bytes=64) for k, width in enumerate(CHUNKS)]
         hw = sb.tile([P, S], U32, name="hw", align_bytes=64)
         hs = sb.tile([P, S], U8, name="hs", align_bytes=64)
 
-        def weave(copy, c0, c1):
+        def weave(copy, k, h, c0):
             copy(
-                woven[:, c0:c1, :].rearrange("p (c i) t -> p c t i", i=4),
-                hid[:, :, c0:c1].rearrange("p t (c i) -> p c t i", i=4),
+                woven[k][:].rearrange("p (c i) t -> p c t i", i=4),
+                hid[:, h, :, c0 : c0 + CHUNKS[k]].rearrange("p t (c i) -> p c t i", i=4),
             )
 
-        weave(nc.vector.tensor_copy, 0, HALF)
-        weave(nc.scalar.copy, HALF, HALF + SCALAR_COLS)
-        weave(nc.vector.tensor_copy, HALF + SCALAR_COLS, S)
+        weave(nc.scalar.copy, 0, 0, 0)
+        for t in range(2, PACK):
+            weigh_cols(t, halves[1])
+        for t in range(2, PACK):
+            hidden_half(t, 1)
+        weave(nc.vector.tensor_copy, 1, 1, 0)
+        weave(nc.scalar.copy, 2, 1, CHUNKS[1])
         c0 = 0
         for k, width in enumerate(CHUNKS):
             cols = slice(c0, c0 + width)
             nc.vector.quantize_mx(
-                out=hw[:, cols].bitcast(FP8X4), scales=hs[:, cols], in_=woven[:, cols, :].rearrange("p c t -> p (c t)")
+                out=hw[:, cols].bitcast(FP8X4), scales=hs[:, cols], in_=woven[k][:].rearrange("p c t -> p (c t)")
             )
             obank = ps.tile([P, width], F32, name=f"o_bank{k}")
             nc.tensor.matmul_mx(

@@ -18,12 +18,14 @@ ACT = mybir.ActivationFunctionType
 
 P = 128
 PACK = 4
-WINDOW = 704
 HALF = S // 2
-CHUNKS = [256, 128, 128]
-PARTNER = "VSSS"
-STRIDE = ["FV","FV","PSV","FV"]
-SKEW = 0.6
+HALVES = [slice(0, HALF), slice(HALF, S)]
+WHOLE = slice(0, S)
+LIST_HALVES = [slice(0, S // 32), slice(S // 32, S // 16)]
+WINDOW = 704
+SCALAR_D2_TILE = 2
+FIRST_LATE_TILE = 2
+CHUNKS = [(0, 0, 256), (1, 0, 128), (1, 128, 128)]
 
 
 def load_scale_rows(queues, plane, rows):
@@ -66,188 +68,189 @@ def tile_picked_yanti_gap_p_kernel(
         nc.sync.dma_start(w2w[:].bitcast(I32), w2_words[0].bitcast(I32))
         load_scale_rows([nc.sync] * 4, w2s, w2_scales[0])
 
-        gw = sb.tile([P, S], U32, name="gw", align_bytes=64)
-        gs = sb.tile([P, S], U8, name="gs", align_bytes=64)
-        nc.vector.tensor_copy(gs[:], xs[:].indirect(offs_t[:]))
+        picked_w = sb.tile([P, S], U32, name="picked_w", align_bytes=64)
+        picked_s = sb.tile([P, S], U8, name="picked_s", align_bytes=64)
+        nc.vector.tensor_copy(picked_s[:], xs[:].indirect(offs_t[:]))
 
-        w1w_t = w1w[:].rearrange("p (m t b) -> p t m b", t=PACK, b=2)
-        w1s_t = w1s[:].rearrange("p (m t) -> p t m", t=PACK)
-        first_w = sb.tile([P, 2, P, 2], U8, name="first_w", align_bytes=64)
+        w1w_dealt = w1w[:].rearrange("p (m t b) -> p t m b", t=PACK, b=2)
+        w1s_dealt = w1s[:].rearrange("p (m t) -> p t m", t=PACK)
+        first_w = sb.tile([P, 1, P, 2], U8, name="first_w", align_bytes=64)
         first_s = sb.tile([P, 2, P], U8, name="first_s", align_bytes=64)
-        nc.vector.tensor_copy(first_w[:], w1w_t[:, 0:2])
-        nc.vector.tensor_copy(gw[:], xw[:].bitcast(U32).indirect(offs_t[:]))
-        nc.vector.tensor_copy(first_s[:], w1s_t[:, 0:2])
+        nc.vector.tensor_copy(first_w[:], w1w_dealt[:, 0:1])
+        nc.vector.tensor_copy(picked_w[:], xw[:].bitcast(U32).indirect(offs_t[:]))
+        nc.vector.tensor_copy(first_s[:], w1s_dealt[:, 0:2])
         rest_s = sb.tile([P, 2, P], U8, name="rest_s", align_bytes=64)
-        nc.vector.tensor_copy(rest_s[:], w1s_t[:, 2:PACK])
-        rest_w = sb.tile([P, 2, P, 2], U8, name="rest_w", tag="w1_bytes", align_bytes=64)
-        nc.vector.tensor_copy(rest_w[:], w1w_t[:, 2:PACK])
+        nc.vector.tensor_copy(rest_s[:], w1s_dealt[:, 2:PACK])
+        rest_w = sb.tile([P, 3, P, 2], U8, name="rest_w", tag="w1_bytes", align_bytes=64)
+        nc.vector.tensor_copy(rest_w[:, 0:1], w1w_dealt[:, 1:2])
+        nc.vector.tensor_copy(rest_w[:, 1:3], w1w_dealt[:, 2:PACK])
 
         nc.scalar.activation(neg_u[:], u[:], ACT.Copy, scale=-1.0)
         nc.scalar.activation(u_times_s[:], u[:], ACT.Copy, scale=float(S))
 
         def first_product(bank, t, cols):
-            words = first_w[:, t] if t < 2 else rest_w[:, t - 2]
+            words = first_w[:, 0] if t == 0 else rest_w[:, t - 1]
             scales = first_s[:, t] if t < 2 else rest_s[:, t - 2]
             nc.tensor.matmul_mx(
                 out=bank,
                 lhsT=words.rearrange("p m b -> p (m b)").bitcast(FP4X4),
                 lhsT_scale=scales,
-                rhs=gw[:, cols].bitcast(FP8X4),
-                rhs_scale=gs[:, cols],
+                rhs=picked_w[:, cols].bitcast(FP8X4),
+                rhs_scale=picked_s[:, cols],
                 start=True,
                 stop=True,
             )
 
-        halves = [slice(0, HALF), slice(HALF, S)]
         half_banks = [ps.tile([P, HALF], F32, name=f"y0_bank{h}") for h in range(2)]
-        banks = [None] + [ps.tile([P, S], F32, name=f"y_bank{t}") for t in range(1, PACK)]
+        banks = {t: ps.tile([P, S], F32, name=f"y_bank{t}") for t in range(1, PACK)}
         for h in range(2):
-            first_product(half_banks[h][:], 0, halves[h])
+            first_product(half_banks[h][:], 0, HALVES[h])
         for t in range(1, PACK):
-            first_product(banks[t][:], t, slice(0, S))
+            first_product(banks[t][:], t, WHOLE)
 
         y = [sb.tile([P, WINDOW], F32, name=f"y{t}") for t in range(PACK)]
         s1 = [sb.tile([P, S], F32, name=f"s1_{t}") for t in range(PACK)]
         ad = [sb.tile([P, WINDOW], F32, name=f"ad{t}") for t in range(PACK)]
-        ad2 = [sb.tile([P, S], F32, name=f"ad_copy{t}") for t in range(PACK)]
+        addend = [sb.tile([P, S], F32, name=f"addend{t}") for t in range(PACK)]
         st = [sb.tile([P, S], F32, name=f"st{t}") for t in range(PACK)]
         th = [sb.tile([P, S], F32, name=f"th{t}") for t in range(PACK)]
         ex = [sb.tile([P, S], F32, name=f"ex{t}") for t in range(PACK)]
-        wy = [sb.tile([P, S], F32, name=f"wy{t}") for t in range(PACK)]
-        tot = sb.tile([P, PACK], F32, name="tot")
-        inv = sb.tile([P, PACK], F32, name="inv")
-        fac = sb.tile([P, PACK], F32, name="fac")
+        weighed = [sb.tile([P, S], F32, name=f"weighed{t}") for t in range(PACK)]
+        total = sb.tile([P, PACK], F32, name="total")
+        inverse = sb.tile([P, PACK], F32, name="inverse")
+        factor = sb.tile([P, PACK], F32, name="factor")
         hid = sb.tile([P, 2, PACK, HALF], BF16, name="hid", align_bytes=64)
 
-        def evac(t):
+        def y_rows(t):
+            return y[0][:, WHOLE] if t == 0 else banks[t][:]
+
+        def pieces(t):
+            return HALVES if t == 0 else [WHOLE]
+
+        def copy_y(t):
             if t == 0:
                 for h in range(2):
-                    nc.scalar.activation(y[0][:, halves[h]], half_banks[h][:], ACT.Copy)
+                    nc.scalar.activation(y[0][:, HALVES[h]], half_banks[h][:], ACT.Copy)
             else:
-                nc.scalar.activation(y[t][:, :S], banks[t][:], ACT.Copy)
+                nc.scalar.activation(y[t][:, WHOLE], banks[t][:], ACT.Copy)
 
-        def y_rows(t):
-            return y[0][:, :S] if t == 0 else banks[t][:]
-
-        def partner(t):
-            if PARTNER[t] == "V":
-                nc.vector.tensor_copy(s1[t][:], y[t][:].indirect(d1_t[:]))
+        def gather_s1(t):
+            if t == 0:
+                for h in range(2):
+                    nc.vector.tensor_copy(s1[0][:, HALVES[h]], y[0][:].indirect(d1_t[:, LIST_HALVES[h]]))
             else:
                 nc.scalar.activation(s1[t][:], y[t][:].indirect(d1_t[:]), ACT.Copy)
 
-        def product(t):
-            nc.vector.tensor_tensor(ad[t][:, :S], y_rows(t), s1[t][:], ALU.mult)
+        def make_ad(t):
+            for cols in pieces(t):
+                nc.vector.tensor_tensor(ad[t][:, cols], y_rows(t)[:, cols], s1[t][:, cols], ALU.mult)
 
-        def dup(t):
-            if STRIDE[t] == "FV":
-                nc.vector.tensor_copy(ad2[t][:], ad[t][:, :S])
-            elif STRIDE[t] == "FS":
-                nc.scalar.activation(ad2[t][:], ad[t][:, :S], ACT.Copy)
-            elif STRIDE[t] == "FD":
-                nc.sync.dma_start(ad2[t][:], ad[t][:, :S])
-            elif STRIDE[t][:2] == "PS":
-                nc.scalar.activation(ad2[t][:], ad[t][:].indirect(d2_t[:]), ACT.Copy)
+        def make_addend(t):
+            if t == SCALAR_D2_TILE:
+                nc.scalar.activation(addend[t][:], ad[t][:].indirect(d2_t[:]), ACT.Copy)
             else:
-                nc.vector.tensor_copy(ad2[t][:], ad[t][:].indirect(d2_t[:]))
+                for cols in pieces(t):
+                    nc.vector.tensor_copy(addend[t][:, cols], ad[t][:, cols])
 
-        def stride_sum(t):
-            if STRIDE[t][0] == "F":
-                nc.vector.tensor_tensor(st[t][:], ad[t][:].indirect(d2_t[:]), ad2[t][:], ALU.add)
-            elif STRIDE[t][2] == "G":
-                nc.gpsimd.tensor_tensor(st[t][:], ad[t][:, :S], ad2[t][:], ALU.add)
-            else:
-                nc.vector.tensor_tensor(st[t][:], ad[t][:, :S], ad2[t][:], ALU.add)
+        def make_st(t):
+            first = ad[t][:, WHOLE] if t == SCALAR_D2_TILE else ad[t][:].indirect(d2_t[:])
+            nc.vector.tensor_tensor(st[t][:], first, addend[t][:], ALU.add)
 
-        def bound(t):
+        def make_tanh(t):
             nc.scalar.activation(th[t][:], st[t][:], ACT.Tanh)
 
-        def exponential(t):
-            nc.scalar.activation(ex[t][:], th[t][:], ACT.Exp, scale=1.5, accum_out=tot[:, t : t + 1])
+        def make_ex(t):
+            nc.scalar.activation(ex[t][:], th[t][:], ACT.Exp, scale=1.5, accum_out=total[:, t : t + 1])
 
-        def factor_cols(t):
-            return slice(0, 2) if t == 1 else slice(t, t + 1)
+        def due(t):
+            if t >= FIRST_LATE_TILE:
+                return range(t, t + 1)
+            return range(FIRST_LATE_TILE) if t == FIRST_LATE_TILE - 1 else range(0)
 
-        def inverse(t):
-            if t > 0:
-                nc.vector.reciprocal(inv[:, factor_cols(t)], tot[:, factor_cols(t)])
+        def make_inverse(t):
+            if due(t):
+                cols = slice(due(t).start, due(t).stop)
+                nc.vector.reciprocal(inverse[:, cols], total[:, cols])
 
-        def factor(t):
-            if t > 0:
-                nc.vector.tensor_tensor(fac[:, factor_cols(t)], inv[:, factor_cols(t)], u_times_s[:, factor_cols(t)], ALU.mult)
+        def make_factor(t):
+            if t >= FIRST_LATE_TILE:
+                nc.scalar.activation(
+                    factor[:, t : t + 1], inverse[:, t : t + 1], ACT.Copy, scale=u_times_s[:, t : t + 1]
+                )
+            elif due(t):
+                cols = slice(due(t).start, due(t).stop)
+                nc.vector.tensor_tensor(factor[:, cols], inverse[:, cols], u_times_s[:, cols], ALU.mult)
 
-        def weigh_cols(t, cols):
+        def weigh(t, cols):
             nc.vector.scalar_tensor_tensor(
-                wy[t][:, cols], ex[t][:, cols], fac[:, t : t + 1], y_rows(t)[:, cols], ALU.mult, ALU.mult
+                weighed[t][:, cols], ex[t][:, cols], factor[:, t : t + 1], y_rows(t)[:, cols], ALU.mult, ALU.mult
             )
 
-        def hidden_half(t, h):
+        def finish(t, first_half, last_half):
+            cols = slice(first_half * HALF, (last_half + 1) * HALF)
             nc.vector.scalar_tensor_tensor(
-                hid[:, h, t, :], s1[t][:, halves[h]], neg_u[:, t : t + 1], wy[t][:, halves[h]], ALU.mult, ALU.add
+                hid[:, first_half : last_half + 1, t, :],
+                s1[t][:, cols].rearrange("p (h c) -> p h c", c=HALF),
+                neg_u[:, t : t + 1],
+                weighed[t][:, cols].rearrange("p (h c) -> p h c", c=HALF),
+                ALU.mult,
+                ALU.add,
             )
 
-        def weigh(t):
-            if t == 1:
-                weigh_cols(0, slice(0, S))
-                weigh_cols(1, slice(0, S))
-            elif t > 1:
-                weigh_cols(t, halves[0])
+        def make_weighed(t):
+            for k in due(t):
+                weigh(k, HALVES[0] if k >= FIRST_LATE_TILE else WHOLE)
 
-        def hidden(t):
-            if t == 1:
-                for k in range(2):
-                    nc.vector.scalar_tensor_tensor(
-                        hid[:, :, k, :],
-                        s1[k][:].rearrange("p (h c) -> p h c", h=2),
-                        neg_u[:, k : k + 1],
-                        wy[k][:].rearrange("p (h c) -> p h c", h=2),
-                        ALU.mult,
-                        ALU.add,
-                    )
-            elif t > 1:
-                hidden_half(t, 0)
+        def make_hid(t):
+            for k in due(t):
+                finish(k, 0, 0 if k >= FIRST_LATE_TILE else 1)
 
-        stages = [evac, partner, product, dup, stride_sum, bound, exponential, inverse, factor, weigh, hidden]
-        steps = [(i + SKEW * t, t, i) for t in range(PACK) for i in range(len(stages))]
-        for step in sorted(steps):
-            stages[step[2]](step[1])
+        stages = [
+            copy_y, gather_s1, make_ad, make_addend, make_st, make_tanh, make_ex,
+            make_inverse, make_factor, make_weighed, make_hid,
+        ]
+        for wave in range(len(stages) + PACK - 1):
+            for t in reversed(range(PACK)):
+                if 0 <= wave - t < len(stages):
+                    stages[wave - t](t)
 
-        woven = [sb.tile([P, width, PACK], BF16, name=f"woven{k}", align_bytes=64) for k, width in enumerate(CHUNKS)]
-        hw = sb.tile([P, S], U32, name="hw", align_bytes=64)
-        hs = sb.tile([P, S], U8, name="hs", align_bytes=64)
+        woven = [sb.tile([P, width, PACK], BF16, name=f"woven{k}", align_bytes=64) for k, (h, c0, width) in enumerate(CHUNKS)]
+        hid_w = sb.tile([P, S], U32, name="hid_w", align_bytes=64)
+        hid_s = sb.tile([P, S], U8, name="hid_s", align_bytes=64)
 
-        def weave(copy, k, h, c0):
+        def weave(copy, k):
+            h, c0, width = CHUNKS[k]
             copy(
                 woven[k][:].rearrange("p (c i) t -> p c t i", i=4),
-                hid[:, h, :, c0 : c0 + CHUNKS[k]].rearrange("p t (c i) -> p c t i", i=4),
+                hid[:, h, :, c0 : c0 + width].rearrange("p t (c i) -> p c t i", i=4),
             )
 
-        weave(nc.scalar.copy, 0, 0, 0)
-        for t in range(2, PACK):
-            weigh_cols(t, halves[1])
-        for t in range(2, PACK):
-            hidden_half(t, 1)
-        weave(nc.vector.tensor_copy, 1, 1, 0)
-        weave(nc.scalar.copy, 2, 1, CHUNKS[1])
-        c0 = 0
-        for k, width in enumerate(CHUNKS):
-            cols = slice(c0, c0 + width)
+        weave(nc.scalar.copy, 0)
+        for t in range(FIRST_LATE_TILE, PACK):
+            weigh(t, HALVES[1])
+        for t in range(FIRST_LATE_TILE, PACK):
+            finish(t, 1, 1)
+        weave(nc.vector.tensor_copy, 1)
+        weave(nc.scalar.copy, 2)
+
+        for k, (h, c0, width) in enumerate(CHUNKS):
+            cols = slice(h * HALF + c0, h * HALF + c0 + width)
             nc.vector.quantize_mx(
-                out=hw[:, cols].bitcast(FP8X4), scales=hs[:, cols], in_=woven[k][:].rearrange("p c t -> p (c t)")
+                out=hid_w[:, cols].bitcast(FP8X4), scales=hid_s[:, cols], in_=woven[k][:].rearrange("p c t -> p (c t)")
             )
-            obank = ps.tile([P, width], F32, name=f"o_bank{k}")
+            out_bank = ps.tile([P, width], F32, name=f"out_bank{k}")
             nc.tensor.matmul_mx(
-                out=obank[:],
+                out=out_bank[:],
                 lhsT=w2w[:].bitcast(FP4X4),
                 lhsT_scale=w2s[:],
-                rhs=hw[:, cols].bitcast(FP8X4),
-                rhs_scale=hs[:, cols],
+                rhs=hid_w[:, cols].bitcast(FP8X4),
+                rhs_scale=hid_s[:, cols],
                 start=True,
                 stop=True,
             )
-            res = sb.tile([P, width], F32, name=f"res{k}")
+            result = sb.tile([P, width], F32, name=f"result{k}")
             if k + 1 < len(CHUNKS):
-                nc.scalar.copy(res[:], obank[:])
+                nc.scalar.copy(result[:], out_bank[:])
             else:
-                nc.vector.tensor_copy(res[:], obank[:])
-            nc.sync.dma_start(out[:, cols], res[:])
-            c0 = c0 + width
+                nc.vector.tensor_copy(result[:], out_bank[:])
+            nc.sync.dma_start(out[:, cols], result[:])

@@ -23,9 +23,9 @@ HALVES = [slice(0, HALF), slice(HALF, S)]
 WHOLE = slice(0, S)
 LIST_HALVES = [slice(0, S // 32), slice(S // 32, S // 16)]
 WINDOW = 704
-SCALAR_D2_TILE = 2
+SCALAR_D2_TILES = (1, 2)
 FIRST_LATE_TILE = 2
-CHUNKS = [(0, 0, 256), (1, 0, 128), (1, 128, 128)]
+CHUNKS = [(0, 0, 128), (0, 128, 128), (1, 0, 128), (1, 128, 128)]
 
 
 def load_scale_rows(queues, plane, rows):
@@ -101,7 +101,7 @@ def tile_picked_yanti_gap_p_kernel(
                 stop=True,
             )
 
-        half_banks = [ps.tile([P, HALF], F32, name=f"y0_bank{h}") for h in range(2)]
+        half_banks = [ps.tile([P, HALF], F32, name=f"y0_bank{h}", tag=f"small_bank{h}") for h in range(2)]
         banks = {t: ps.tile([P, S], F32, name=f"y_bank{t}") for t in range(1, PACK)}
         for h in range(2):
             first_product(half_banks[h][:], 0, HALVES[h])
@@ -138,6 +138,8 @@ def tile_picked_yanti_gap_p_kernel(
             if t == 0:
                 for h in range(2):
                     nc.vector.tensor_copy(s1[0][:, HALVES[h]], y[0][:].indirect(d1_t[:, LIST_HALVES[h]]))
+            elif t == 1:
+                nc.vector.tensor_copy(s1[1][:], y[1][:].indirect(d1_t[:]))
             else:
                 nc.scalar.activation(s1[t][:], y[t][:].indirect(d1_t[:]), ACT.Copy)
 
@@ -146,14 +148,14 @@ def tile_picked_yanti_gap_p_kernel(
                 nc.vector.tensor_tensor(ad[t][:, cols], y_rows(t)[:, cols], s1[t][:, cols], ALU.mult)
 
         def make_addend(t):
-            if t == SCALAR_D2_TILE:
+            if t in SCALAR_D2_TILES:
                 nc.scalar.activation(addend[t][:], ad[t][:].indirect(d2_t[:]), ACT.Copy)
             else:
                 for cols in pieces(t):
                     nc.vector.tensor_copy(addend[t][:, cols], ad[t][:, cols])
 
         def make_st(t):
-            first = ad[t][:, WHOLE] if t == SCALAR_D2_TILE else ad[t][:].indirect(d2_t[:])
+            first = ad[t][:, WHOLE] if t in SCALAR_D2_TILES else ad[t][:].indirect(d2_t[:])
             nc.vector.tensor_tensor(st[t][:], first, addend[t][:], ALU.add)
 
         def make_tanh(t):
@@ -226,19 +228,20 @@ def tile_picked_yanti_gap_p_kernel(
             )
 
         weave(nc.scalar.copy, 0)
+        weave(nc.scalar.copy, 1)
         for t in range(FIRST_LATE_TILE, PACK):
             weigh(t, HALVES[1])
         for t in range(FIRST_LATE_TILE, PACK):
             finish(t, 1, 1)
-        weave(nc.vector.tensor_copy, 1)
-        weave(nc.scalar.copy, 2)
+        weave(nc.vector.tensor_copy, 2)
+        weave(nc.scalar.copy, 3)
 
         for k, (h, c0, width) in enumerate(CHUNKS):
             cols = slice(h * HALF + c0, h * HALF + c0 + width)
             nc.vector.quantize_mx(
                 out=hid_w[:, cols].bitcast(FP8X4), scales=hid_s[:, cols], in_=woven[k][:].rearrange("p c t -> p (c t)")
             )
-            out_bank = ps.tile([P, width], F32, name=f"out_bank{k}")
+            out_bank = ps.tile([P, width], F32, name=f"out_bank{k}", tag=f"small_bank{k}")
             nc.tensor.matmul_mx(
                 out=out_bank[:],
                 lhsT=w2w[:].bitcast(FP4X4),

from contextlib import ExitStack

import concourse.mybir as mybir

K, T, S, H, N = 512, 1024, 512, 512, 128
FLOPS = 2 * K * H * S + 2 * H * N * S

F32 = mybir.dt.float32
BF16 = mybir.dt.bfloat16
I32 = mybir.dt.int32
U32 = mybir.dt.uint32
U16 = mybir.dt.uint16
U8 = mybir.dt.uint8
FP8X4 = mybir.dt.float8_e4m3fn_x4
FP4X4 = mybir.dt.float4_e2m1fn_x4
ALU = mybir.AluOpType
ACT = mybir.ActivationFunctionType

P = 128
PACK = 4
HALF = S // 2
HALVES = [slice(0, HALF), slice(HALF, S)]
WHOLE = slice(0, S)
LIST_HALVES = [slice(0, S // 32), slice(S // 32, S // 16)]
WINDOW = 704
SCALAR_D2_TILES = (1, 2)
FIRST_LATE_TILE = 2
CHUNKS = [(0, 0, 128), (0, 128, 128), (1, 0, 128), (1, 128, 128)]


def load_scale_rows(queues, plane, rows):
    for q, queue in enumerate(queues):
        words = rows[4 * q : 4 * q + 4, :].bitcast(I32)
        queue.dma_start(
            plane[32 * q : 32 * q + 32, :].bitcast(I32), words.unsqueeze(0).to_broadcast([8, 4, words.shape[1]])
        )


def tile_picked_yanti_gap_p_kernel(
    tc, x_words, x_scales, w1_words, w1_scales, unit, w2_words, w2_scales, offs, d1, d2, out
):
    nc = tc.nc
    with ExitStack() as ctx:
        sb = ctx.enter_context(tc.tile_pool(name="sb", bufs=1))
        ps = ctx.enter_context(tc.psum_pool(name="ps", bufs=1))

        offs_t = sb.tile([P, S // 16], U16, name="offs_t")
        d1_t = sb.tile([P, S // 16], U16, name="d1_t")
        d2_t = sb.tile([P, S // 16], U16, name="d2_t")
        xw = sb.tile([P, T], I32, name="xw", align_bytes=64)
        xs = sb.tile([P, T], U8, name="xs", align_bytes=64)
        w1w = sb.tile([P, 2 * H], U8, name="w1w", align_bytes=64)
        w1s = sb.tile([P, H], U8, name="w1s", tag="w1_bytes", align_bytes=64)
        w2w = sb.tile([P, 2 * N], U8, name="w2w", align_bytes=64)
        w2s = sb.tile([P, N], U8, name="w2s", align_bytes=64)
        u = sb.tile([P, PACK], F32, name="u")
        neg_u = sb.tile([P, PACK], F32, name="neg_u")
        u_times_s = sb.tile([P, PACK], F32, name="u_times_s")

        nc.sync.dma_start(offs_t[:], offs)
        load_scale_rows([nc.sync, nc.scalar, nc.sync, nc.scalar], xs, x_scales[0])
        nc.sync.dma_start(w1w[:].bitcast(I32), w1_words[0].bitcast(I32))
        nc.scalar.dma_start(xw[:], x_words[0].rearrange("p c r -> p (c r)").bitcast(I32))
        load_scale_rows([nc.sync] * 4, w1s, w1_scales[0])
        nc.sync.dma_start(d1_t[:], d1)
        nc.sync.dma_start(u[:], unit.rearrange("(p t) o -> p (t o)", t=PACK))
        nc.sync.dma_start(d2_t[:], d2)
        nc.sync.dma_start(w2w[:].bitcast(I32), w2_words[0].bitcast(I32))
        load_scale_rows([nc.sync] * 4, w2s, w2_scales[0])

        picked_w = sb.tile([P, S], U32, name="picked_w", align_bytes=64)
        picked_s = sb.tile([P, S], U8, name="picked_s", align_bytes=64)
        nc.vector.tensor_copy(picked_s[:], xs[:].indirect(offs_t[:]))

        w1w_dealt = w1w[:].rearrange("p (m t b) -> p t m b", t=PACK, b=2)
        w1s_dealt = w1s[:].rearrange("p (m t) -> p t m", t=PACK)
        first_w = sb.tile([P, 1, P, 2], U8, name="first_w", align_bytes=64)
        first_s = sb.tile([P, 2, P], U8, name="first_s", align_bytes=64)
        nc.vector.tensor_copy(first_w[:], w1w_dealt[:, 0:1])
        nc.vector.tensor_copy(picked_w[:], xw[:].bitcast(U32).indirect(offs_t[:]))
        nc.vector.tensor_copy(first_s[:], w1s_dealt[:, 0:2])
        rest_s = sb.tile([P, 2, P], U8, name="rest_s", align_bytes=64)
        nc.vector.tensor_copy(rest_s[:], w1s_dealt[:, 2:PACK])
        rest_w = sb.tile([P, 3, P, 2], U8, name="rest_w", tag="w1_bytes", align_bytes=64)
        nc.vector.tensor_copy(rest_w[:, 0:1], w1w_dealt[:, 1:2])
        nc.vector.tensor_copy(rest_w[:, 1:3], w1w_dealt[:, 2:PACK])

        nc.scalar.activation(neg_u[:], u[:], ACT.Copy, scale=-1.0)
        nc.scalar.activation(u_times_s[:], u[:], ACT.Copy, scale=float(S))

        def first_product(bank, t, cols):
            words = first_w[:, 0] if t == 0 else rest_w[:, t - 1]
            scales = first_s[:, t] if t < 2 else rest_s[:, t - 2]
            nc.tensor.matmul_mx(
                out=bank,
                lhsT=words.rearrange("p m b -> p (m b)").bitcast(FP4X4),
                lhsT_scale=scales,
                rhs=picked_w[:, cols].bitcast(FP8X4),
                rhs_scale=picked_s[:, cols],
                start=True,
                stop=True,
            )

        half_banks = [ps.tile([P, HALF], F32, name=f"y0_bank{h}", tag=f"small_bank{h}") for h in range(2)]
        banks = {t: ps.tile([P, S], F32, name=f"y_bank{t}") for t in range(1, PACK)}
        for h in range(2):
            first_product(half_banks[h][:], 0, HALVES[h])
        for t in range(1, PACK):
            first_product(banks[t][:], t, WHOLE)

        y = [sb.tile([P, WINDOW], F32, name=f"y{t}") for t in range(PACK)]
        s1 = [sb.tile([P, S], F32, name=f"s1_{t}") for t in range(PACK)]
        ad = [sb.tile([P, WINDOW], F32, name=f"ad{t}") for t in range(PACK)]
        addend = [sb.tile([P, S], F32, name=f"addend{t}") for t in range(PACK)]
        st = [sb.tile([P, S], F32, name=f"st{t}") for t in range(PACK)]
        th = [sb.tile([P, S], F32, name=f"th{t}") for t in range(PACK)]
        ex = [sb.tile([P, S], F32, name=f"ex{t}") for t in range(PACK)]
        weighed = [sb.tile([P, S], F32, name=f"weighed{t}") for t in range(PACK)]
        total = sb.tile([P, PACK], F32, name="total")
        inverse = sb.tile([P, PACK], F32, name="inverse")
        factor = sb.tile([P, PACK], F32, name="factor")
        hid = sb.tile([P, 2, PACK, HALF], BF16, name="hid", align_bytes=64)

        def y_rows(t):
            return y[0][:, WHOLE] if t == 0 else banks[t][:]

        def pieces(t):
            return HALVES if t == 0 else [WHOLE]

        def copy_y(t):
            if t == 0:
                for h in range(2):
                    nc.scalar.activation(y[0][:, HALVES[h]], half_banks[h][:], ACT.Copy)
            else:
                nc.scalar.activation(y[t][:, WHOLE], banks[t][:], ACT.Copy)

        def gather_s1(t):
            if t == 0:
                for h in range(2):
                    nc.vector.tensor_copy(s1[0][:, HALVES[h]], y[0][:].indirect(d1_t[:, LIST_HALVES[h]]))
            elif t == 1:
                nc.vector.tensor_copy(s1[1][:], y[1][:].indirect(d1_t[:]))
            else:
                nc.scalar.activation(s1[t][:], y[t][:].indirect(d1_t[:]), ACT.Copy)

        def make_ad(t):
            for cols in pieces(t):
                nc.vector.tensor_tensor(ad[t][:, cols], y_rows(t)[:, cols], s1[t][:, cols], ALU.mult)

        def make_addend(t):
            if t in SCALAR_D2_TILES:
                nc.scalar.activation(addend[t][:], ad[t][:].indirect(d2_t[:]), ACT.Copy)
            else:
                for cols in pieces(t):
                    nc.vector.tensor_copy(addend[t][:, cols], ad[t][:, cols])

        def make_st(t):
            first = ad[t][:, WHOLE] if t in SCALAR_D2_TILES else ad[t][:].indirect(d2_t[:])
            nc.vector.tensor_tensor(st[t][:], first, addend[t][:], ALU.add)

        def make_tanh(t):
            nc.scalar.activation(th[t][:], st[t][:], ACT.Tanh)

        def make_ex(t):
            nc.scalar.activation(ex[t][:], th[t][:], ACT.Exp, scale=1.5, accum_out=total[:, t : t + 1])

        def due(t):
            if t >= FIRST_LATE_TILE:
                return range(t, t + 1)
            return range(FIRST_LATE_TILE) if t == FIRST_LATE_TILE - 1 else range(0)

        def make_inverse(t):
            if due(t):
                cols = slice(due(t).start, due(t).stop)
                nc.vector.reciprocal(inverse[:, cols], total[:, cols])

        def make_factor(t):
            if t >= FIRST_LATE_TILE:
                nc.scalar.activation(
                    factor[:, t : t + 1], inverse[:, t : t + 1], ACT.Copy, scale=u_times_s[:, t : t + 1]
                )
            elif due(t):
                cols = slice(due(t).start, due(t).stop)
                nc.vector.tensor_tensor(factor[:, cols], inverse[:, cols], u_times_s[:, cols], ALU.mult)

        def weigh(t, cols):
            nc.vector.scalar_tensor_tensor(
                weighed[t][:, cols], ex[t][:, cols], factor[:, t : t + 1], y_rows(t)[:, cols], ALU.mult, ALU.mult
            )

        def finish(t, first_half, last_half):
            cols = slice(first_half * HALF, (last_half + 1) * HALF)
            nc.vector.scalar_tensor_tensor(
                hid[:, first_half : last_half + 1, t, :],
                s1[t][:, cols].rearrange("p (h c) -> p h c", c=HALF),
                neg_u[:, t : t + 1],
                weighed[t][:, cols].rearrange("p (h c) -> p h c", c=HALF),
                ALU.mult,
                ALU.add,
            )

        def make_weighed(t):
            for k in due(t):
                weigh(k, HALVES[0] if k >= FIRST_LATE_TILE else WHOLE)

        def make_hid(t):
            for k in due(t):
                finish(k, 0, 0 if k >= FIRST_LATE_TILE else 1)

        stages = [
            copy_y, gather_s1, make_ad, make_addend, make_st, make_tanh, make_ex,
            make_inverse, make_factor, make_weighed, make_hid,
        ]
        for wave in range(len(stages) + PACK - 1):
            for t in reversed(range(PACK)):
                if 0 <= wave - t < len(stages):
                    stages[wave - t](t)

        woven = [sb.tile([P, width, PACK], BF16, name=f"woven{k}", align_bytes=64) for k, (h, c0, width) in enumerate(CHUNKS)]
        hid_w = sb.tile([P, S], U32, name="hid_w", align_bytes=64)
        hid_s = sb.tile([P, S], U8, name="hid_s", align_bytes=64)

        def weave(copy, k):
            h, c0, width = CHUNKS[k]
            copy(
                woven[k][:].rearrange("p (c i) t -> p c t i", i=4),
                hid[:, h, :, c0 : c0 + width].rearrange("p t (c i) -> p c t i", i=4),
            )

        weave(nc.scalar.copy, 0)
        weave(nc.scalar.copy, 1)
        for t in range(FIRST_LATE_TILE, PACK):
            weigh(t, HALVES[1])
        for t in range(FIRST_LATE_TILE, PACK):
            finish(t, 1, 1)
        weave(nc.vector.tensor_copy, 2)
        weave(nc.scalar.copy, 3)

        for k, (h, c0, width) in enumerate(CHUNKS):
            cols = slice(h * HALF + c0, h * HALF + c0 + width)
            nc.vector.quantize_mx(
                out=hid_w[:, cols].bitcast(FP8X4), scales=hid_s[:, cols], in_=woven[k][:].rearrange("p c t -> p (c t)")
            )
            out_bank = ps.tile([P, width], F32, name=f"out_bank{k}", tag=f"small_bank{k}")
            nc.tensor.matmul_mx(
                out=out_bank[:],
                lhsT=w2w[:].bitcast(FP4X4),
                lhsT_scale=w2s[:],
                rhs=hid_w[:, cols].bitcast(FP8X4),
                rhs_scale=hid_s[:, cols],
                start=True,
                stop=True,
            )
            result = sb.tile([P, width], F32, name=f"result{k}")
            if k + 1 < len(CHUNKS):
                nc.scalar.copy(result[:], out_bank[:])
            else:
                nc.vector.tensor_copy(result[:], out_bank[:])
            nc.sync.dma_start(out[:, cols], result[:])
